import numpy as np
import ml_dtypes


def mxq(x, axis, fmt="e4m3"):
    dtype, down = {"e4m3": (ml_dtypes.float8_e4m3fn, 7), "e5m2": (ml_dtypes.float8_e5m2, 14)}[fmt]
    v = np.moveaxis(np.asarray(x, np.float32).astype(ml_dtypes.bfloat16).astype(np.float64), axis, -1)
    blocks = v.reshape(v.shape[:-1] + (-1, 32))
    amax = np.abs(blocks).max(-1, keepdims=True)
    byte = np.maximum(np.where(amax > 0, np.frexp(amax)[1] - 1 + 127, 0) - down, 1)
    scale = np.exp2(byte - 127.0)
    codes = (blocks / scale).astype(np.float32).astype(dtype).astype(np.float64)
    return np.moveaxis((codes * scale).reshape(v.shape), -1, axis)


WIDE = False


def mx_kscale(k):
    if not WIDE:
        return np.ones(k)
    levels = np.array([10, -10, 5, -5, 0])
    if k % 512:
        return np.exp2(np.random.permutation(np.resize(levels, k // 32))).repeat(32)
    a = np.empty((k // 512, 16))
    for p in range(k // 512):
        a[p, :8] = np.random.permutation(np.resize(levels, 8))
        for g in range(8):
            far = levels[np.abs(levels - a[p, g]) >= 10]
            a[p, g + 8] = far[np.random.randint(len(far))]
    return np.exp2(a.ravel()).repeat(32)


def f64(x):
    return np.asarray(x).astype(np.float64)


def striped(idx):
    return np.tile(idx.reshape(-1, 16).T, (8, 1)).astype(np.uint16)


def unstriped(offs):
    return offs[:16].T.reshape(-1).astype(np.int64)


E2M1 = np.array([0.0, 0.5, 1.0, 1.5, 2.0, 3.0, 4.0, 6.0, -0.0, -0.5, -1.0, -1.5, -2.0, -3.0, -4.0, -6.0])


def pack_weight(w, fmt):
    k, n = w.shape
    w = f64(np.asarray(w, np.float32).astype(ml_dtypes.bfloat16)).reshape(k // 32, 32, n)
    amax = np.abs(w).max(1)
    if fmt == "e4m3":
        byte = np.frexp(amax)[1] - 1 + 127 - 7
    else:
        mant, ex = np.frexp(amax / 6.0)
        byte = np.where(mant > 0.5, ex, ex - 1) + 127
    byte = np.clip(np.where(amax > 0, byte, 1), 1, 254)
    scaled = (w * np.exp2(127.0 - byte)[:, None, :]).reshape(k, n).astype(np.float32)
    by_word = np.ascontiguousarray(scaled.reshape(k // 512, 128, 4, n).transpose(0, 1, 3, 2))
    if fmt == "e4m3":
        words = by_word.astype(ml_dtypes.float8_e4m3fn).view(np.uint8)
    else:
        c = by_word.astype(ml_dtypes.float4_e2m1fn).view(np.uint8) & 0xF
        words = (c[..., 0::2] | (c[..., 1::2] << 4)).reshape(k // 512, 128, 2 * n)
    return np.ascontiguousarray(words), np.ascontiguousarray(byte.astype(np.uint8).reshape(k // 512, 16, n))


def unpack_weight(words, scales, fmt):
    g, _, n = scales.shape
    words = np.ascontiguousarray(words).reshape(g, 128, n, -1)
    if fmt == "e4m3":
        vals = words.view(ml_dtypes.float8_e4m3fn).astype(np.float64)
    else:
        nib = np.empty((g, 128, n, 4), np.uint8)
        nib[..., 0::2] = words & 0xF
        nib[..., 1::2] = words >> 4
        vals = E2M1[nib]
    vals = vals * np.repeat(np.exp2(scales.astype(np.float64) - 127.0), 8, axis=1)[..., None]
    return vals.transpose(0, 1, 3, 2).reshape(g * 512, n)


def gelu(v):
    return 0.5 * v * (1.0 + np.tanh(np.sqrt(2.0 / np.pi) * (v + 0.044715 * v**3)))


def twice(P):
    return np.random.permutation(np.repeat(np.arange(P), 2))


K, T, S, H, P = 512, 4096, 1024, 1024, 512

def setup_inputs():
    n = np.random.standard_normal
    s = mx_kscale(K)[:, None]
    u = mx_kscale(H)[:, None]
    d = {}
    d["tab_words"], d["tab_scales"] = pack_weight(n((K, T)) * s, "e4m3")
    d["offs"] = striped(np.random.permutation(T)[:S])
    d["pos1"] = striped(np.random.permutation(S)[:P])
    d["pos2"] = striped(np.random.permutation(S)[:P])
    d["pos3"] = striped(twice(P))
    d["wa"] = (n((K, H)) / K**0.5 / s).astype(np.float32)
    d["wb_words"], d["wb_scales"] = pack_weight(0.7 * n((K, H)) / K**0.5 / s, "e2m1")
    d["wy_words"], d["wy_scales"] = pack_weight(3.0 * n((H, H)) / H**0.5 / u, "e4m3")
    d["thr"] = (0.7 * n(H)).astype(np.float32)
    d["gt"] = (np.exp(0.3 * n(H)) * u[:, 0]).astype(np.float32)
    d["gh"] = np.exp(0.3 * n(H)).astype(np.float32)
    d["bh"] = (0.7 * n(H)).astype(np.float32)
    return d

def reference(tab_words, tab_scales, offs, pos1, pos2, pos3, wa, wb_words, wb_scales,
              wy_words, wy_scales, thr, gt, gh, bh):
    v = unpack_weight(tab_words, tab_scales, "e4m3")[:, unstriped(offs)]
    wb = unpack_weight(wb_words, wb_scales, "e2m1")
    wy = unpack_weight(wy_words, wy_scales, "e4m3")
    lo = mxq(f64(wa), 0, "e4m3").T @ v
    h = np.maximum(lo, f64(thr)[:, None]) - (wb.T @ v)
    x = np.tanh(h[:, unstriped(pos1)] - h[:, unstriped(pos2)]) * f64(gt)[:, None]
    y = wy.T @ mxq(x, 0, "e4m3")
    up = 1.0 / (1.0 + np.exp(-y[:, unstriped(pos3)]))
    return (h * f64(gh)[:, None] - f64(bh)[:, None]) * up

@@ -1,0 +1,307 @@
+from contextlib import ExitStack
+
+import concourse.mybir as mybir
+
+K, T, S, H, PAIRS = 512, 4096, 1024, 1024, 512
+FLOPS = 2 * (2 * K * H * S + H * H * PAIRS)
+
+F32 = mybir.dt.float32
+BF16 = mybir.dt.bfloat16
+I32 = mybir.dt.int32
+U32 = mybir.dt.uint32
+U16 = mybir.dt.uint16
+U8 = mybir.dt.uint8
+E4M3X4 = mybir.dt.float8_e4m3fn_x4
+E2M1X4 = mybir.dt.float4_e2m1fn_x4
+ALU = mybir.AluOpType
+ACT = mybir.ActivationFunctionType
+
+P = 128
+PACK = 4
+PASS = P * PACK
+BANK = 512
+BLOCKS = H // PASS
+SLICES = BLOCKS * PACK
+LIST_ROWS = 16
+PIECE = 256
+
+
+def tile_list_flue_chamber_scorer_kernel(
+    tc, tab_words, tab_scales, offs, pos1, pos2, pos3, wa, wb_words, wb_scales,
+    wy_words, wy_scales, thr, gt, gh, bh, out,
+):
+    nc = tc.nc
+    with ExitStack() as ctx:
+        lists = ctx.enter_context(tc.tile_pool(name="lists", bufs=1))
+        keep = ctx.enter_context(tc.tile_pool(name="keep", bufs=1))
+        ring = ctx.enter_context(tc.tile_pool(name="ring", bufs=2))
+        psum = ctx.enter_context(tc.psum_pool(name="psum", bufs=2))
+
+        def load_list(src, name):
+            tile = lists.tile(list(src.shape), U16, name=name)
+            nc.sync.dma_start(tile[:], src)
+            return tile
+
+        def load_rows(vec, name):
+            tile = keep.tile([P, BLOCKS, PACK], F32, name=name)
+            nc.gpsimd.dma_start(tile[:], vec.rearrange("(b p t) -> p b t", b=BLOCKS, t=PACK))
+            return tile[:].rearrange("p b t -> p (b t)")
+
+        tab_s = keep.tile([P, T], U8, name="tab_s", align_bytes=64)
+        wb_s_raw = keep.tile([P, H], U8, name="wb_s_raw", align_bytes=64)
+        wy_s_raw = keep.tile([P, H], U8, name="wy_s_raw", align_bytes=64)
+        nc.vector.memset(tab_s[:].bitcast(I32), 0)
+        nc.gpsimd.memset(wb_s_raw[:].bitcast(I32), 0)
+        nc.vector.memset(wy_s_raw[:].bitcast(I32), 0)
+
+        offs_t = load_list(offs, "offs_t")
+        pos1_t = load_list(pos1, "pos1_t")
+        pos2_t = load_list(pos2, "pos2_t")
+        pos3_t = load_list(pos3, "pos3_t")
+        for q in range(4):
+            nc.scalar.dma_start(tab_s[32 * q : 32 * q + 4, :].bitcast(I32), tab_scales[0, 4 * q : 4 * q + 4, :].bitcast(I32))
+        for q in range(4):
+            nc.gpsimd.dma_start(wb_s_raw[32 * q : 32 * q + 4, :].bitcast(I32), wb_scales[0, 4 * q : 4 * q + 4, :].bitcast(I32))
+        wb_raw = keep.tile([P, 2 * H], U8, name="wb_raw", align_bytes=64)
+        nc.sync.dma_start(wb_raw[:].bitcast(I32), wb_words[0].bitcast(I32))
+        tab_w = keep.tile([P, T], I32, name="tab_w", align_bytes=64)
+        nc.sync.dma_start(tab_w[:], tab_words[0].rearrange("p n i -> p (n i)").bitcast(I32))
+
+        def load_wa(piece):
+            raw = ring.tile([P, PACK, PIECE], F32, name="wa_raw", tag="raw")
+            cols = slice(piece * PIECE, (piece + 1) * PIECE)
+            nc.sync.dma_start(raw[:], wa[:, cols].rearrange("(p j) c -> p j c", j=PACK))
+            return raw
+
+        wa_raw = [load_wa(0), load_wa(1)]
+        bh_t = load_rows(bh, "bh_t")
+        thr_t = load_rows(thr, "thr_t")
+        gt_t = load_rows(gt, "gt_t")
+        gh_t = load_rows(gh, "gh_t")
+        for q in range(4):
+            nc.gpsimd.dma_start(wy_s_raw[32 * q : 32 * q + 8, :].bitcast(I32), wy_scales[:, 4 * q : 4 * q + 4, :].bitcast(I32))
+
+        neg_bh = keep.tile([P, SLICES], F32, name="neg_bh")
+        nc.scalar.activation(neg_bh[:], bh_t, ACT.Copy, scale=-1.0)
+
+        wb_w = keep.tile([P, 2 * H], U8, name="wb_w", align_bytes=64)
+        wb_s = keep.tile([P, H], U8, name="wb_s", align_bytes=64)
+        nc.vector.tensor_copy(
+            wb_w[:].bitcast(U16).rearrange("p (b t c i) -> p b c t i", b=BLOCKS, t=PACK, i=8),
+            wb_raw[:].bitcast(U16).rearrange("p (b c i t) -> p b c t i", b=BLOCKS, t=PACK, i=8),
+        )
+
+        v_w = [keep.tile([P, BANK], U32, name=f"v_w{j}", align_bytes=64) for j in range(S // BANK)]
+        v_s = keep.tile([P, S], U8, name="v_s", align_bytes=64)
+        nc.vector.tensor_copy(v_s[:], tab_s[:].indirect(offs_t[:]))
+        nc.vector.tensor_copy(
+            wb_s[:].rearrange("p (b t c i) -> p b c t i", b=BLOCKS, t=PACK, i=16),
+            wb_s_raw[:].rearrange("p (b c i t) -> p b c t i", b=BLOCKS, t=PACK, i=16),
+        )
+        cols_per_bank = BANK // LIST_ROWS
+        for j in range(S // BANK):
+            nc.vector.tensor_copy(
+                v_w[j][:], tab_w[:].bitcast(U32).indirect(offs_t[:, j * cols_per_bank : (j + 1) * cols_per_bank])
+            )
+
+        wa_w = keep.tile([P, H], U32, name="wa_w", align_bytes=64)
+        wa_s = keep.tile([P, H], U8, name="wa_s", align_bytes=64)
+        wa_bf = [keep.tile([P, PACK, P, PACK], BF16, name=f"wa_bf{b}", align_bytes=64) for b in range(BLOCKS)]
+
+        def round_wa(piece, copy):
+            b, half = divmod(piece, PASS // PIECE)
+            qs = slice(half * PIECE // PACK, (half + 1) * PIECE // PACK)
+            copy(
+                wa_bf[b][:, :, qs, :].rearrange("p t q j -> p q t j"),
+                wa_raw[piece][:].rearrange("p j (q t) -> p q t j", t=PACK),
+            )
+
+        def quantise_wa(b, t0, t1):
+            cols = slice(b * PASS + t0 * P, b * PASS + t1 * P)
+            nc.vector.quantize_mx(
+                out=wa_w[:, cols].bitcast(E4M3X4), scales=wa_s[:, cols],
+                in_=wa_bf[b][:, t0:t1].rearrange("p t q j -> p (t q j)"),
+            )
+
+        round_wa(0, nc.scalar.copy)
+        round_wa(1, nc.vector.tensor_copy)
+        quantise_wa(0, 0, 1)
+        quantise_wa(0, 1, PACK)
+        wa_raw.append(load_wa(2))
+        wa_raw.append(load_wa(3))
+
+        h = [keep.tile([P, S], F32, name=f"h{n}") for n in range(SLICES)]
+        x_w = [keep.tile([P, PAIRS], U32, name=f"x_w{b}", align_bytes=64) for b in range(BLOCKS)]
+        x_s = [keep.tile([P, PAIRS], U8, name=f"x_s{b}", align_bytes=64) for b in range(BLOCKS)]
+        x_bf = [keep.tile([P, PACK, PAIRS], BF16, name=f"x_bf{b}", align_bytes=64) for b in range(BLOCKS)]
+        x_il = [keep.tile([P, PAIRS, PACK], BF16, name=f"x_il{b}", align_bytes=64) for b in range(BLOCKS)]
+        staged = {}
+        picked = {}
+
+        def products(n):
+            cols = slice(n * P, (n + 1) * P)
+            for j in range(S // BANK):
+                js = slice(j * BANK, (j + 1) * BANK)
+                hb_ps = psum.tile([P, BANK], F32, name="hb_ps", tag=f"hb{j}")
+                nc.tensor.matmul_mx(
+                    out=hb_ps[:], lhsT=wb_w[:, 2 * n * P : 2 * (n + 1) * P].bitcast(E2M1X4), lhsT_scale=wb_s[:, cols],
+                    rhs=v_w[j][:].bitcast(E4M3X4), rhs_scale=v_s[:, js], start=True, stop=True,
+                )
+                lo_ps = psum.tile([P, BANK], F32, name="lo_ps", tag=f"lo{j}")
+                nc.tensor.matmul_mx(
+                    out=lo_ps[:], lhsT=wa_w[:, cols].bitcast(E4M3X4), lhsT_scale=wa_s[:, cols],
+                    rhs=v_w[j][:].bitcast(E4M3X4), rhs_scale=v_s[:, js], start=True, stop=True,
+                )
+                hb_sb = ring.tile([P, BANK], F32, name="hb_sb", tag=f"hb_sb{j}")
+                nc.scalar.copy(hb_sb[:], hb_ps[:])
+                staged[(n, j)] = (lo_ps, hb_sb)
+
+        def join(n, j):
+            lo_ps, hb_sb = staged[(n, j)]
+            nc.vector.scalar_tensor_tensor(
+                h[n][:, j * BANK : (j + 1) * BANK], lo_ps[:], thr_t[:, n : n + 1], hb_sb[:], ALU.max, ALU.subtract
+            )
+
+        def pair_tiles(n):
+            if n == SLICES - 1:
+                second = keep.tile([P, PAIRS], F32, name="second", tag="late_words", align_bytes=64)
+                diff = keep.tile([P, PAIRS], F32, name="diff", tag="late_scales", align_bytes=64)
+            else:
+                second = ring.tile([P, PAIRS], F32, name="second")
+                diff = ring.tile([P, PAIRS], F32, name="diff")
+            bounded = ring.tile([P, PAIRS], F32, name="bounded")
+            picked[n] = (second, diff, bounded)
+
+        def list_cols(ms):
+            return slice(ms.start // LIST_ROWS, ms.stop // LIST_ROWS)
+
+        def pick_second(n, ms):
+            nc.vector.tensor_copy(picked[n][0][:, ms], h[n][:].indirect(pos2_t[:, list_cols(ms)]))
+
+        def pair(n, ms):
+            b, t = divmod(n, PACK)
+            second, diff, bounded = picked[n]
+            nc.vector.tensor_tensor(diff[:, ms], h[n][:].indirect(pos1_t[:, list_cols(ms)]), second[:, ms], ALU.subtract)
+            nc.scalar.activation(bounded[:, ms], diff[:, ms], ACT.Tanh)
+            nc.scalar.activation(x_bf[b][:, t, ms], bounded[:, ms], ACT.Copy, scale=gt_t[:, n : n + 1])
+
+        def weave_x(b, ms, copy):
+            copy(
+                x_il[b][:, ms, :].rearrange("p (c i) t -> p c t i", i=4),
+                x_bf[b][:, :, ms].rearrange("p t (c i) -> p c t i", i=4),
+            )
+
+        def quantise_x(b, ms):
+            nc.vector.quantize_mx(
+                out=x_w[b][:, ms].bitcast(E4M3X4), scales=x_s[b][:, ms],
+                in_=x_il[b][:, ms, :].rearrange("p m t -> p (m t)"),
+            )
+
+        pages = {}
+
+        def shift_h(n):
+            page = ring.tile([P, PAIRS + S], F32, name="page", bufs=4)
+            nc.scalar.activation(
+                page[:, PAIRS:], h[n][:], ACT.Identity, bias=neg_bh[:, n : n + 1], scale=gh_t[:, n : n + 1]
+            )
+            pages[n] = page
+
+        whole = slice(0, PAIRS)
+        halves = [slice(0, PAIRS // 2), slice(PAIRS // 2, PAIRS)]
+        wy_raw = []
+        products(0)
+        join(0, 0)
+        join(0, 1)
+        for n in range(SLICES):
+            pair_tiles(n)
+            if n + 1 < SLICES:
+                products(n + 1)
+                join(n + 1, 0)
+                pick_second(n, whole)
+                join(n + 1, 1)
+                pair(n, whole)
+            else:
+                pick_second(n, halves[0])
+                pick_second(n, halves[1])
+                pair(n, halves[0])
+                pair(n, halves[1])
+            if n < 2:
+                round_wa(2 + n, nc.scalar.copy)
+                raw = ring.tile([P, H], I32, name="wy_raw", tag="raw")
+                nc.sync.dma_start(raw[:], wy_words[n].rearrange("p c i -> p (c i)").bitcast(I32))
+                wy_raw.append(raw)
+            if n == 1:
+                quantise_wa(1, 0, PACK)
+            if n == PACK:
+                weave_x(0, whole, nc.scalar.copy)
+            if n == PACK + 1:
+                quantise_x(0, whole)
+            if n in (2, 6):
+                shift_h(n // 4)
+
+        wy_w = keep.tile([P, BLOCKS, H], I32, name="wy_w", tag="late_words", align_bytes=64)
+        wy_s = keep.tile([P, H], U8, name="wy_s", tag="late_scales", align_bytes=64)
+
+        def deal_wy(b):
+            cols = slice(b * PASS, (b + 1) * PASS)
+            for a in range(BLOCKS):
+                nc.vector.tensor_copy(
+                    wy_w[:, a, cols].rearrange("p (t c i) -> p c t i", t=PACK, i=4),
+                    wy_raw[a][:, cols].rearrange("p (c i t) -> p c t i", t=PACK, i=4),
+                )
+
+        deal_wy(0)
+        weave_x(1, halves[0], nc.vector.tensor_copy)
+        nc.vector.tensor_copy(
+            wy_s[:].rearrange("p (b t c i) -> p b c t i", b=BLOCKS, t=PACK, i=16),
+            wy_s_raw[:].rearrange("p (b c i t) -> p b c t i", b=BLOCKS, t=PACK, i=16),
+        )
+        quantise_x(1, halves[0])
+        weave_x(1, halves[1], nc.vector.tensor_copy)
+        quantise_x(1, halves[1])
+        deal_wy(1)
+
+        out_rows = out.rearrange("(b p t) j -> b t p j", b=BLOCKS, t=PACK)
+        lifted = {}
+
+        def second_stage(n):
+            cols = slice(n * P, (n + 1) * P)
+            if n not in pages:
+                shift_h(n)
+            page = pages[n]
+            y_ps = psum.tile([P, PAIRS], F32, name="y_ps", tag=f"hb{n % 2}")
+            for a in range(BLOCKS):
+                nc.tensor.matmul_mx(
+                    out=y_ps[:], lhsT=wy_w[:, a, cols].bitcast(E4M3X4), lhsT_scale=wy_s[4 * a : P, cols],
+                    rhs=x_w[a][:].bitcast(E4M3X4), rhs_scale=x_s[a][:], start=(a == 0), stop=(a == BLOCKS - 1),
+                )
+            nc.scalar.copy(page[:, :PAIRS], y_ps[:])
+
+        def lift(n, js):
+            up = lifted[n]
+            nc.vector.tensor_copy(up[:, js], pages[n][:].indirect(pos3_t[:, list_cols(js)]))
+            nc.scalar.activation(up[:, js], up[:, js], ACT.Sigmoid)
+
+        def finish(n, js):
+            b, t = divmod(n, PACK)
+            up = lifted[n]
+            nc.vector.tensor_tensor(up[:, js], up[:, js], pages[n][:, PAIRS + js.start : PAIRS + js.stop], ALU.mult)
+            nc.sync.dma_start(out_rows[b, t, :, js], up[:, js])
+
+        row = slice(0, S)
+        last_parts = [slice(0, 512), slice(512, 768), slice(768, 1024)]
+        second_stage(0)
+        for n in range(SLICES):
+            lifted[n] = ring.tile([P, S], F32, name="up", bufs=4)
+            if n + 1 < SLICES:
+                second_stage(n + 1)
+                lift(n, row)
+                if n > 0:
+                    finish(n - 1, row)
+            else:
+                lift(n, last_parts[0])
+                finish(n - 1, row)
+                lift(n, last_parts[1])
+                lift(n, last_parts[2])
+                for js in last_parts:
+                    finish(n, js)

@@ -49,19 +49,17 @@ def tile_list_flue_chamber_scorer_kernel(
 
         tab_s = keep.tile([P, T], U8, name="tab_s", align_bytes=64)
         wb_s_raw = keep.tile([P, H], U8, name="wb_s_raw", align_bytes=64)
-        wy_s_raw = keep.tile([P, H], U8, name="wy_s_raw", align_bytes=64)
-        nc.vector.memset(tab_s[:].bitcast(I32), 0)
+        v_s = keep.tile([P, S], U8, name="v_s", align_bytes=64)
         nc.gpsimd.memset(wb_s_raw[:].bitcast(I32), 0)
-        nc.vector.memset(wy_s_raw[:].bitcast(I32), 0)
+        nc.gpsimd.memset(tab_s[:, : T // 2].bitcast(I32), 0)
+        nc.vector.memset(tab_s[:, T // 2 :].bitcast(I32), 0)
+        bh_t = load_rows(bh, "bh_t")
+        nc.vector.memset(v_s[:].bitcast(I32), 0)
 
         offs_t = load_list(offs, "offs_t")
-        pos1_t = load_list(pos1, "pos1_t")
-        pos2_t = load_list(pos2, "pos2_t")
-        pos3_t = load_list(pos3, "pos3_t")
+        nc.scalar.dma_start(tab_s[0:P:8, :].bitcast(I32), tab_scales[0].bitcast(I32))
         for q in range(4):
-            nc.scalar.dma_start(tab_s[32 * q : 32 * q + 4, :].bitcast(I32), tab_scales[0, 4 * q : 4 * q + 4, :].bitcast(I32))
-        for q in range(4):
-            nc.gpsimd.dma_start(wb_s_raw[32 * q : 32 * q + 4, :].bitcast(I32), wb_scales[0, 4 * q : 4 * q + 4, :].bitcast(I32))
+            nc.sync.dma_start(wb_s_raw[32 * q : 32 * q + 4, :].bitcast(I32), wb_scales[0, 4 * q : 4 * q + 4, :].bitcast(I32))
         wb_raw = keep.tile([P, 2 * H], U8, name="wb_raw", align_bytes=64)
         nc.sync.dma_start(wb_raw[:].bitcast(I32), wb_words[0].bitcast(I32))
         tab_w = keep.tile([P, T], I32, name="tab_w", align_bytes=64)
@@ -74,12 +72,12 @@ def tile_list_flue_chamber_scorer_kernel(
             return raw
 
         wa_raw = [load_wa(0), load_wa(1)]
-        bh_t = load_rows(bh, "bh_t")
+        pos2_t = load_list(pos2, "pos2_t")
+        pos1_t = load_list(pos1, "pos1_t")
+        pos3_t = load_list(pos3, "pos3_t")
         thr_t = load_rows(thr, "thr_t")
         gt_t = load_rows(gt, "gt_t")
         gh_t = load_rows(gh, "gh_t")
-        for q in range(4):
-            nc.gpsimd.dma_start(wy_s_raw[32 * q : 32 * q + 8, :].bitcast(I32), wy_scales[:, 4 * q : 4 * q + 4, :].bitcast(I32))
 
         neg_bh = keep.tile([P, SLICES], F32, name="neg_bh")
         nc.scalar.activation(neg_bh[:], bh_t, ACT.Copy, scale=-1.0)
@@ -92,12 +90,17 @@ def tile_list_flue_chamber_scorer_kernel(
         )
 
         v_w = [keep.tile([P, BANK], U32, name=f"v_w{j}", align_bytes=64) for j in range(S // BANK)]
-        v_s = keep.tile([P, S], U8, name="v_s", align_bytes=64)
-        nc.vector.tensor_copy(v_s[:], tab_s[:].indirect(offs_t[:]))
         nc.vector.tensor_copy(
             wb_s[:].rearrange("p (b t c i) -> p b c t i", b=BLOCKS, t=PACK, i=16),
             wb_s_raw[:].rearrange("p (b c i t) -> p b c t i", b=BLOCKS, t=PACK, i=16),
         )
+        v_s_rows = keep.tile([P, S], U8, name="v_s_rows", align_bytes=64)
+        nc.vector.tensor_copy(v_s_rows[:], tab_s[:].indirect(offs_t[:]))
+        for q in range(4):
+            nc.scalar.dma_start(v_s[32 * q : 32 * q + 4, :].bitcast(I32), v_s_rows[32 * q : 32 * q + 32 : 8, :].bitcast(I32))
+        wy_s_raw = wb_s_raw
+        for q in range(4):
+            nc.gpsimd.dma_start(wy_s_raw[32 * q : 32 * q + 8, :].bitcast(I32), wy_scales[:, 4 * q : 4 * q + 4, :].bitcast(I32))
         cols_per_bank = BANK // LIST_ROWS
         for j in range(S // BANK):
             nc.vector.tensor_copy(
@@ -200,7 +203,7 @@ def tile_list_flue_chamber_scorer_kernel(
         pages = {}
 
         def shift_h(n):
-            page = ring.tile([P, PAIRS + S], F32, name="page", bufs=4)
+            page = ring.tile([P, PAIRS + S], F32, name="page", bufs=6)
             nc.scalar.activation(
                 page[:, PAIRS:], h[n][:], ACT.Identity, bias=neg_bh[:, n : n + 1], scale=gh_t[:, n : n + 1]
             )
@@ -236,8 +239,8 @@ def tile_list_flue_chamber_scorer_kernel(
                 weave_x(0, whole, nc.scalar.copy)
             if n == PACK + 1:
                 quantise_x(0, whole)
-            if n in (2, 6):
-                shift_h(n // 4)
+            if n in (2, 3, 5, 6):
+                shift_h(len(pages))
 
         wy_w = keep.tile([P, BLOCKS, H], I32, name="wy_w", tag="late_words", align_bytes=64)
         wy_s = keep.tile([P, H], U8, name="wy_s", tag="late_scales", align_bytes=64)
@@ -282,10 +285,10 @@ def tile_list_flue_chamber_scorer_kernel(
             nc.vector.tensor_copy(up[:, js], pages[n][:].indirect(pos3_t[:, list_cols(js)]))
             nc.scalar.activation(up[:, js], up[:, js], ACT.Sigmoid)
 
-        def finish(n, js):
+        def finish(n, js, engine):
             b, t = divmod(n, PACK)
             up = lifted[n]
-            nc.vector.tensor_tensor(up[:, js], up[:, js], pages[n][:, PAIRS + js.start : PAIRS + js.stop], ALU.mult)
+            engine.tensor_tensor(up[:, js], up[:, js], pages[n][:, PAIRS + js.start : PAIRS + js.stop], ALU.mult)
             nc.sync.dma_start(out_rows[b, t, :, js], up[:, js])
 
         row = slice(0, S)
@@ -295,13 +298,15 @@ def tile_list_flue_chamber_scorer_kernel(
             lifted[n] = ring.tile([P, S], F32, name="up", bufs=4)
             if n + 1 < SLICES:
                 second_stage(n + 1)
-                lift(n, row)
-                if n > 0:
-                    finish(n - 1, row)
+                lift(n, slice(0, BANK))
+                lift(n, slice(BANK, S))
+                if n + 2 < SLICES:
+                    finish(n, row, nc.gpsimd)
+                else:
+                    finish(n, slice(0, BANK), nc.gpsimd)
+                    finish(n, slice(BANK, S), nc.gpsimd)
             else:
-                lift(n, last_parts[0])
-                finish(n - 1, row)
-                lift(n, last_parts[1])
-                lift(n, last_parts[2])
                 for js in last_parts:
-                    finish(n, js)
+                    lift(n, js)
+                for js in last_parts:
+                    finish(n, js, nc.vector)

@@ -24,6 +24,9 @@ BLOCKS = H // PASS
 SLICES = BLOCKS * PACK
 LIST_ROWS = 16
 PIECE = 256
+FUSED_FROM = 7
+SHIFTS_ON_GPSIMD = 5
+WEAVE_AT = 4
 
 
 def tile_list_flue_chamber_scorer_kernel(
@@ -66,7 +69,7 @@ def tile_list_flue_chamber_scorer_kernel(
         nc.sync.dma_start(tab_w[:], tab_words[0].rearrange("p n i -> p (n i)").bitcast(I32))
 
         def load_wa(piece):
-            raw = ring.tile([P, PACK, PIECE], F32, name="wa_raw", tag="raw")
+            raw = keep.tile([P, PACK, PIECE], F32, name="wa_raw", tag=f"stage{piece}")
             cols = slice(piece * PIECE, (piece + 1) * PIECE)
             nc.sync.dma_start(raw[:], wa[:, cols].rearrange("(p j) c -> p j c", j=PACK))
             return raw
@@ -130,14 +133,20 @@ def tile_list_flue_chamber_scorer_kernel(
         round_wa(1, nc.vector.tensor_copy)
         quantise_wa(0, 0, 1)
         quantise_wa(0, 1, PACK)
-        wa_raw.append(load_wa(2))
-        wa_raw.append(load_wa(3))
 
         h = [keep.tile([P, S], F32, name=f"h{n}") for n in range(SLICES)]
-        x_w = [keep.tile([P, PAIRS], U32, name=f"x_w{b}", align_bytes=64) for b in range(BLOCKS)]
+        x_w = {1: keep.tile([P, PAIRS], U32, name="x_w1", align_bytes=64)}
         x_s = [keep.tile([P, PAIRS], U8, name=f"x_s{b}", align_bytes=64) for b in range(BLOCKS)]
-        x_bf = [keep.tile([P, PACK, PAIRS], BF16, name=f"x_bf{b}", align_bytes=64) for b in range(BLOCKS)]
-        x_il = [keep.tile([P, PAIRS, PACK], BF16, name=f"x_il{b}", align_bytes=64) for b in range(BLOCKS)]
+        whole = slice(0, PAIRS)
+        parts = [slice(0, 256), slice(256, 384), slice(384, 512)]
+        x_parts = [[whole], parts]
+        x_pairs = {}
+        x_il = {}
+        for b in range(BLOCKS):
+            for ms in x_parts[b]:
+                width = ms.stop - ms.start
+                x_pairs[(b, ms.start)] = keep.tile([P, 2, width, 2], BF16, name=f"x_pairs{b}_{ms.start}", align_bytes=64)
+                x_il[(b, ms.start)] = keep.tile([P, width, PACK], BF16, name=f"x_il{b}_{ms.start}", align_bytes=64)
         staged = {}
         picked = {}
 
@@ -155,24 +164,28 @@ def tile_list_flue_chamber_scorer_kernel(
                     out=lo_ps[:], lhsT=wa_w[:, cols].bitcast(E4M3X4), lhsT_scale=wa_s[:, cols],
                     rhs=v_w[j][:].bitcast(E4M3X4), rhs_scale=v_s[:, js], start=True, stop=True,
                 )
-                hb_sb = ring.tile([P, BANK], F32, name="hb_sb", tag=f"hb_sb{j}")
+                if n == 0:
+                    hb_sb = keep.tile([P, BANK], F32, name="hb_sb", tag=f"stage{2 + j}")
+                else:
+                    hb_sb = ring.tile([P, BANK], F32, name="hb_sb", tag=f"hb_sb{j}")
                 nc.scalar.copy(hb_sb[:], hb_ps[:])
                 staged[(n, j)] = (lo_ps, hb_sb)
 
         def join(n, j):
-            lo_ps, hb_sb = staged[(n, j)]
-            nc.vector.scalar_tensor_tensor(
-                h[n][:, j * BANK : (j + 1) * BANK], lo_ps[:], thr_t[:, n : n + 1], hb_sb[:], ALU.max, ALU.subtract
-            )
+            lo, hb_sb = staged[(n, j)]
+            dst = h[n][:, j * BANK : (j + 1) * BANK]
+            nc.vector.scalar_tensor_tensor(dst, lo[:], thr_t[:, n : n + 1], hb_sb[:], ALU.max, ALU.subtract)
 
         def pair_tiles(n):
             if n == SLICES - 1:
-                second = keep.tile([P, PAIRS], F32, name="second", tag="late_words", align_bytes=64)
-                diff = keep.tile([P, PAIRS], F32, name="diff", tag="late_scales", align_bytes=64)
+                second = keep.tile([P, PAIRS], F32, name="second", tag="late_codes", align_bytes=64)
             else:
                 second = ring.tile([P, PAIRS], F32, name="second")
-                diff = ring.tile([P, PAIRS], F32, name="diff")
-            bounded = ring.tile([P, PAIRS], F32, name="bounded")
+            diff = ring.tile([P, PAIRS], F32, name="diff")
+            if n >= SLICES - 2:
+                bounded = keep.tile([P, PAIRS], F32, name="bounded", tag="late_page")
+            else:
+                bounded = ring.tile([P, PAIRS], F32, name="bounded")
             picked[n] = (second, diff, bounded)
 
         def list_cols(ms):
@@ -184,101 +197,135 @@ def tile_list_flue_chamber_scorer_kernel(
         def pair(n, ms):
             b, t = divmod(n, PACK)
             second, diff, bounded = picked[n]
-            nc.vector.tensor_tensor(diff[:, ms], h[n][:].indirect(pos1_t[:, list_cols(ms)]), second[:, ms], ALU.subtract)
+            if n >= FUSED_FROM:
+                nc.vector.tensor_tensor(diff[:, ms], h[n][:].indirect(pos1_t[:, list_cols(ms)]), second[:, ms], ALU.subtract)
+            else:
+                first = ring.tile([P, PAIRS], F32, name="first")
+                nc.vector.tensor_copy(first[:], h[n][:].indirect(pos1_t[:]))
+                nc.gpsimd.tensor_tensor(diff[:], first[:], second[:], ALU.subtract)
             nc.scalar.activation(bounded[:, ms], diff[:, ms], ACT.Tanh)
-            nc.scalar.activation(x_bf[b][:, t, ms], bounded[:, ms], ACT.Copy, scale=gt_t[:, n : n + 1])
+            for part in x_parts[b]:
+                if ms.start <= part.start < ms.stop:
+                    nc.scalar.activation(
+                        x_pairs[(b, part.start)][:, t // 2, :, t % 2], bounded[:, part], ACT.Copy, scale=gt_t[:, n : n + 1]
+                    )
 
         def weave_x(b, ms, copy):
             copy(
-                x_il[b][:, ms, :].rearrange("p (c i) t -> p c t i", i=4),
-                x_bf[b][:, :, ms].rearrange("p t (c i) -> p c t i", i=4),
+                x_il[(b, ms.start)][:].bitcast(F32),
+                x_pairs[(b, ms.start)][:].rearrange("p u m e -> p u (m e)").bitcast(F32).rearrange("p u m -> p m u"),
             )
 
         def quantise_x(b, ms):
             nc.vector.quantize_mx(
                 out=x_w[b][:, ms].bitcast(E4M3X4), scales=x_s[b][:, ms],
-                in_=x_il[b][:, ms, :].rearrange("p m t -> p (m t)"),
+                in_=x_il[(b, ms.start)][:].rearrange("p m t -> p (m t)"),
             )
 
         pages = {}
 
-        def shift_h(n):
-            page = ring.tile([P, PAIRS + S], F32, name="page", bufs=6)
-            nc.scalar.activation(
-                page[:, PAIRS:], h[n][:], ACT.Identity, bias=neg_bh[:, n : n + 1], scale=gh_t[:, n : n + 1]
-            )
-            pages[n] = page
+        def shift_h(n, js):
+            if n == 5:
+                pages[n] = keep.tile([P, PAIRS + S], F32, name="page", tag="late_page")
+            if n not in pages:
+                pages[n] = ring.tile([P, PAIRS + S], F32, name="page", bufs=5)
+            dst = pages[n][:, PAIRS + js.start : PAIRS + js.stop]
+            if n < SHIFTS_ON_GPSIMD:
+                nc.gpsimd.tensor_scalar(
+                    dst, h[n][:, js], gh_t[:, n : n + 1], neg_bh[:, n : n + 1], ALU.mult, ALU.add
+                )
+            else:
+                nc.scalar.activation(
+                    dst, h[n][:, js], ACT.Identity, bias=neg_bh[:, n : n + 1], scale=gh_t[:, n : n + 1]
+                )
 
-        whole = slice(0, PAIRS)
-        halves = [slice(0, PAIRS // 2), slice(PAIRS // 2, PAIRS)]
+        row = slice(0, S)
+        wy_w = [keep.tile([P, BLOCKS, PASS], I32, name=f"wy_w{b}", align_bytes=64) for b in range(BLOCKS)]
+        wy_s = keep.tile([P, H], U8, name="wy_s", align_bytes=64)
+
+        def deal_wy(b, engine):
+            cols = slice(b * PASS, (b + 1) * PASS)
+            for a in range(BLOCKS):
+                engine.tensor_copy(
+                    wy_w[b][:, a, :].rearrange("p (t c i) -> p c t i", t=PACK, i=4),
+                    wy_raw[a][:, cols].rearrange("p (c i t) -> p c t i", t=PACK, i=4),
+                )
+
         wy_raw = []
         products(0)
         join(0, 0)
         join(0, 1)
+        products(1)
+        for a in range(BLOCKS):
+            wa_raw.append(load_wa(2 + a))
+            round_wa(2 + a, nc.scalar.copy)
+            raw = keep.tile([P, H], I32, name="wy_raw", tag=f"stage{2 + a}")
+            nc.sync.dma_start(raw[:], wy_words[a].rearrange("p c i -> p (c i)").bitcast(I32))
+            wy_raw.append(raw)
         for n in range(SLICES):
             pair_tiles(n)
+            if n + 2 < SLICES:
+                products(n + 2)
             if n + 1 < SLICES:
-                products(n + 1)
                 join(n + 1, 0)
                 pick_second(n, whole)
                 join(n + 1, 1)
                 pair(n, whole)
             else:
-                pick_second(n, halves[0])
-                pick_second(n, halves[1])
-                pair(n, halves[0])
-                pair(n, halves[1])
-            if n < 2:
-                round_wa(2 + n, nc.scalar.copy)
-                raw = ring.tile([P, H], I32, name="wy_raw", tag="raw")
-                nc.sync.dma_start(raw[:], wy_words[n].rearrange("p c i -> p (c i)").bitcast(I32))
-                wy_raw.append(raw)
-            if n == 1:
+                pick_second(n, parts[0])
+                pick_second(n, parts[1])
+                pair(n, parts[0])
+                pair(n, parts[1])
+                pick_second(n, parts[2])
+                pair(n, parts[2])
+            if n == 0:
                 quantise_wa(1, 0, PACK)
-            if n == PACK:
+            if n == WEAVE_AT:
                 weave_x(0, whole, nc.scalar.copy)
-            if n == PACK + 1:
-                quantise_x(0, whole)
-            if n in (2, 3, 5, 6):
-                shift_h(len(pages))
-
-        wy_w = keep.tile([P, BLOCKS, H], I32, name="wy_w", tag="late_words", align_bytes=64)
-        wy_s = keep.tile([P, H], U8, name="wy_s", tag="late_scales", align_bytes=64)
-
-        def deal_wy(b):
-            cols = slice(b * PASS, (b + 1) * PASS)
-            for a in range(BLOCKS):
-                nc.vector.tensor_copy(
-                    wy_w[:, a, cols].rearrange("p (t c i) -> p c t i", t=PACK, i=4),
-                    wy_raw[a][:, cols].rearrange("p (c i t) -> p c t i", t=PACK, i=4),
+            if n < 5:
+                shift_h(n, row)
+            if n == 0:
+                nc.gpsimd.tensor_copy(
+                    wy_s[:].rearrange("p (b t c i) -> p b c t i", b=BLOCKS, t=PACK, i=16),
+                    wy_s_raw[:].rearrange("p (b c i t) -> p b c t i", b=BLOCKS, t=PACK, i=16),
                 )
+            if n == 5:
+                deal_wy(0, nc.gpsimd)
+                deal_wy(1, nc.gpsimd)
 
-        deal_wy(0)
-        weave_x(1, halves[0], nc.vector.tensor_copy)
-        nc.vector.tensor_copy(
-            wy_s[:].rearrange("p (b t c i) -> p b c t i", b=BLOCKS, t=PACK, i=16),
-            wy_s_raw[:].rearrange("p (b c i t) -> p b c t i", b=BLOCKS, t=PACK, i=16),
-        )
-        quantise_x(1, halves[0])
-        weave_x(1, halves[1], nc.vector.tensor_copy)
-        quantise_x(1, halves[1])
-        deal_wy(1)
+        shift_h(5, row)
+        x_w[0] = keep.tile([P, PAIRS], U32, name="x_w0", tag="late_codes", align_bytes=64)
+        quantise_x(0, whole)
+        weave_x(1, parts[0], nc.vector.tensor_copy)
+        weave_x(1, parts[1], nc.vector.tensor_copy)
+        quantise_x(1, parts[0])
+        weave_x(1, parts[2], nc.vector.tensor_copy)
+        quantise_x(1, parts[1])
+        quantise_x(1, parts[2])
 
         out_rows = out.rearrange("(b p t) j -> b t p j", b=BLOCKS, t=PACK)
         lifted = {}
 
         def second_stage(n):
             cols = slice(n * P, (n + 1) * P)
-            if n not in pages:
-                shift_h(n)
             page = pages[n]
-            y_ps = psum.tile([P, PAIRS], F32, name="y_ps", tag=f"hb{n % 2}")
-            for a in range(BLOCKS):
-                nc.tensor.matmul_mx(
-                    out=y_ps[:], lhsT=wy_w[:, a, cols].bitcast(E4M3X4), lhsT_scale=wy_s[4 * a : P, cols],
-                    rhs=x_w[a][:].bitcast(E4M3X4), rhs_scale=x_s[a][:], start=(a == 0), stop=(a == BLOCKS - 1),
-                )
-            nc.scalar.copy(page[:, :PAIRS], y_ps[:])
+            b, t = divmod(n, PACK)
+            if n == 0:
+                pieces = list(zip(parts, ("hb0", "lo0", "lo0"), [(0, 1)] * 3))
+            else:
+                pieces = [(whole, "lo0", (1, 0))]
+            for ms, bank, passes in pieces:
+                y_ps = psum.tile([P, BANK], F32, name="y_ps", tag=bank)
+                width = ms.stop - ms.start
+                for a in passes:
+                    nc.tensor.matmul_mx(
+                        out=y_ps[:, :width], lhsT=wy_w[b][:, a, t * P : (t + 1) * P].bitcast(E4M3X4),
+                        lhsT_scale=wy_s[4 * a : P, cols],
+                        rhs=x_w[a][:, ms].bitcast(E4M3X4), rhs_scale=x_s[a][:, ms],
+                        start=(a == passes[0]), stop=(a == passes[-1]),
+                    )
+                copy = nc.vector.tensor_copy if n == 0 and ms != parts[0] else nc.scalar.copy
+                copy(page[:, ms], y_ps[:, :width])
 
         def lift(n, js):
             up = lifted[n]
@@ -291,22 +338,26 @@ def tile_list_flue_chamber_scorer_kernel(
             engine.tensor_tensor(up[:, js], up[:, js], pages[n][:, PAIRS + js.start : PAIRS + js.stop], ALU.mult)
             nc.sync.dma_start(out_rows[b, t, :, js], up[:, js])
 
-        row = slice(0, S)
         last_parts = [slice(0, 512), slice(512, 768), slice(768, 1024)]
+        first_parts = [slice(0, 256), slice(256, S)]
         second_stage(0)
         for n in range(SLICES):
             lifted[n] = ring.tile([P, S], F32, name="up", bufs=4)
             if n + 1 < SLICES:
                 second_stage(n + 1)
-                lift(n, slice(0, BANK))
-                lift(n, slice(BANK, S))
+                if 2 <= n < 6:
+                    late, half = divmod(n - 2, 2)
+                    shift_h(6 + late, slice(half * BANK, (half + 1) * BANK))
+                for js in (first_parts if n == 0 else (slice(0, BANK), slice(BANK, S))):
+                    lift(n, js)
                 if n + 2 < SLICES:
                     finish(n, row, nc.gpsimd)
+
                 else:
                     finish(n, slice(0, BANK), nc.gpsimd)
-                    finish(n, slice(BANK, S), nc.gpsimd)
             else:
                 for js in last_parts:
                     lift(n, js)
+                finish(n - 1, slice(BANK, S), nc.vector)
                 for js in last_parts:
                     finish(n, js, nc.vector)

@@ -112,7 +112,7 @@ def tile_list_flue_chamber_scorer_kernel(
 
         wa_w = keep.tile([P, H], U32, name="wa_w", align_bytes=64)
         wa_s = keep.tile([P, H], U8, name="wa_s", align_bytes=64)
-        wa_bf = [keep.tile([P, PACK, P, PACK], BF16, name=f"wa_bf{b}", align_bytes=64) for b in range(BLOCKS)]
+        wa_bf = [keep.tile([P, PACK, P, PACK], BF16, name="wa_bf", tag=f"wa_bf{b}", align_bytes=64) for b in range(BLOCKS)]
 
         def round_wa(piece, copy):
             b, half = divmod(piece, PASS // PIECE)
@@ -133,9 +133,15 @@ def tile_list_flue_chamber_scorer_kernel(
         round_wa(1, nc.vector.tensor_copy)
         quantise_wa(0, 0, 1)
         quantise_wa(0, 1, PACK)
+        wy_s = keep.tile([P, H], U8, name="wy_s", tag="wa_bf0", align_bytes=64)
+        nc.vector.tensor_copy(
+            wy_s[:].rearrange("p (b t c i) -> p b c t i", b=BLOCKS, t=PACK, i=16),
+            wy_s_raw[:].rearrange("p (b c i t) -> p b c t i", b=BLOCKS, t=PACK, i=16),
+        )
 
         h = [keep.tile([P, S], F32, name=f"h{n}") for n in range(SLICES)]
-        x_w = {1: keep.tile([P, PAIRS], U32, name="x_w1", align_bytes=64)}
+        x_w1 = keep.tile([P, PAIRS], I32, name="x_w1", align_bytes=64)
+        x_w = {1: x_w1[:]}
         x_s = [keep.tile([P, PAIRS], U8, name=f"x_s{b}", align_bytes=64) for b in range(BLOCKS)]
         whole = slice(0, PAIRS)
         parts = [slice(0, 256), slice(256, 384), slice(384, 512)]
@@ -146,7 +152,7 @@ def tile_list_flue_chamber_scorer_kernel(
             for ms in x_parts[b]:
                 width = ms.stop - ms.start
                 x_pairs[(b, ms.start)] = keep.tile([P, 2, width, 2], BF16, name=f"x_pairs{b}_{ms.start}", align_bytes=64)
-                x_il[(b, ms.start)] = keep.tile([P, width, PACK], BF16, name=f"x_il{b}_{ms.start}", align_bytes=64)
+                x_il[(b, ms.start)] = keep.tile([P, width, PACK], BF16, name="x_il", tag=f"x_il{b}_{ms.start}", align_bytes=64)
         staged = {}
         picked = {}
 
@@ -180,7 +186,7 @@ def tile_list_flue_chamber_scorer_kernel(
             if n == SLICES - 1:
                 second = keep.tile([P, PAIRS], F32, name="second", tag="late_codes", align_bytes=64)
             else:
-                second = ring.tile([P, PAIRS], F32, name="second")
+                second = ring.tile([P, PAIRS], F32, name="second", bufs=3)
             diff = ring.tile([P, PAIRS], F32, name="diff")
             if n >= SLICES - 2:
                 bounded = keep.tile([P, PAIRS], F32, name="bounded", tag="late_page")
@@ -200,7 +206,7 @@ def tile_list_flue_chamber_scorer_kernel(
             if n >= FUSED_FROM:
                 nc.vector.tensor_tensor(diff[:, ms], h[n][:].indirect(pos1_t[:, list_cols(ms)]), second[:, ms], ALU.subtract)
             else:
-                first = ring.tile([P, PAIRS], F32, name="first")
+                first = ring.tile([P, PAIRS], F32, name="first", bufs=3)
                 nc.vector.tensor_copy(first[:], h[n][:].indirect(pos1_t[:]))
                 nc.gpsimd.tensor_tensor(diff[:], first[:], second[:], ALU.subtract)
             nc.scalar.activation(bounded[:, ms], diff[:, ms], ACT.Tanh)
@@ -240,13 +246,12 @@ def tile_list_flue_chamber_scorer_kernel(
                 )
 
         row = slice(0, S)
-        wy_w = [keep.tile([P, BLOCKS, PASS], I32, name=f"wy_w{b}", align_bytes=64) for b in range(BLOCKS)]
-        wy_s = keep.tile([P, H], U8, name="wy_s", align_bytes=64)
+        wy_w = {}
 
-        def deal_wy(b, engine):
+        def deal_wy(b):
             cols = slice(b * PASS, (b + 1) * PASS)
             for a in range(BLOCKS):
-                engine.tensor_copy(
+                nc.vector.tensor_copy(
                     wy_w[b][:, a, :].rearrange("p (t c i) -> p c t i", t=PACK, i=4),
                     wy_raw[a][:, cols].rearrange("p (c i t) -> p c t i", t=PACK, i=4),
                 )
@@ -284,24 +289,22 @@ def tile_list_flue_chamber_scorer_kernel(
                 weave_x(0, whole, nc.scalar.copy)
             if n < 5:
                 shift_h(n, row)
-            if n == 0:
-                nc.gpsimd.tensor_copy(
-                    wy_s[:].rearrange("p (b t c i) -> p b c t i", b=BLOCKS, t=PACK, i=16),
-                    wy_s_raw[:].rearrange("p (b c i t) -> p b c t i", b=BLOCKS, t=PACK, i=16),
-                )
-            if n == 5:
-                deal_wy(0, nc.gpsimd)
-                deal_wy(1, nc.gpsimd)
 
         shift_h(5, row)
-        x_w[0] = keep.tile([P, PAIRS], U32, name="x_w0", tag="late_codes", align_bytes=64)
+        late = keep.tile([P, 1 + BLOCKS, PASS], I32, name="late", tag="late_codes", align_bytes=64)
+        x_w[0] = late[:, 0, :]
+        wy_w[0] = late[:, 1:, :]
         quantise_x(0, whole)
+        deal_wy(0)
         weave_x(1, parts[0], nc.vector.tensor_copy)
         weave_x(1, parts[1], nc.vector.tensor_copy)
         quantise_x(1, parts[0])
         weave_x(1, parts[2], nc.vector.tensor_copy)
         quantise_x(1, parts[1])
         quantise_x(1, parts[2])
+        wy_w1 = keep.tile([P, BLOCKS, PASS], I32, name="wy_w1", tag=f"x_il1_{parts[2].start}", align_bytes=64)
+        wy_w[1] = wy_w1[:]
+        deal_wy(1)
 
         out_rows = out.rearrange("(b p t) j -> b t p j", b=BLOCKS, t=PACK)
         lifted = {}

from contextlib import ExitStack

import concourse.mybir as mybir

K, T, S, H, PAIRS = 512, 4096, 1024, 1024, 512
FLOPS = 2 * (2 * K * H * S + H * H * PAIRS)

F32 = mybir.dt.float32
BF16 = mybir.dt.bfloat16
I32 = mybir.dt.int32
U32 = mybir.dt.uint32
U16 = mybir.dt.uint16
U8 = mybir.dt.uint8
E4M3X4 = mybir.dt.float8_e4m3fn_x4
E2M1X4 = mybir.dt.float4_e2m1fn_x4
ALU = mybir.AluOpType
ACT = mybir.ActivationFunctionType

P = 128
PACK = 4
PASS = P * PACK
BANK = 512
BLOCKS = H // PASS
SLICES = BLOCKS * PACK
LIST_ROWS = 16
PIECE = 256
FUSED_FROM = 7
SHIFTS_ON_GPSIMD = 5
WEAVE_AT = 4


def tile_list_flue_chamber_scorer_kernel(
    tc, tab_words, tab_scales, offs, pos1, pos2, pos3, wa, wb_words, wb_scales,
    wy_words, wy_scales, thr, gt, gh, bh, out,
):
    nc = tc.nc
    with ExitStack() as ctx:
        lists = ctx.enter_context(tc.tile_pool(name="lists", bufs=1))
        keep = ctx.enter_context(tc.tile_pool(name="keep", bufs=1))
        ring = ctx.enter_context(tc.tile_pool(name="ring", bufs=2))
        psum = ctx.enter_context(tc.psum_pool(name="psum", bufs=2))

        def load_list(src, name):
            tile = lists.tile(list(src.shape), U16, name=name)
            nc.sync.dma_start(tile[:], src)
            return tile

        def load_rows(vec, name):
            tile = keep.tile([P, BLOCKS, PACK], F32, name=name)
            nc.gpsimd.dma_start(tile[:], vec.rearrange("(b p t) -> p b t", b=BLOCKS, t=PACK))
            return tile[:].rearrange("p b t -> p (b t)")

        tab_s = keep.tile([P, T], U8, name="tab_s", align_bytes=64)
        wb_s_raw = keep.tile([P, H], U8, name="wb_s_raw", align_bytes=64)
        v_s = keep.tile([P, S], U8, name="v_s", align_bytes=64)
        nc.gpsimd.memset(wb_s_raw[:].bitcast(I32), 0)
        nc.gpsimd.memset(tab_s[:, : T // 2].bitcast(I32), 0)
        nc.vector.memset(tab_s[:, T // 2 :].bitcast(I32), 0)
        bh_t = load_rows(bh, "bh_t")
        nc.vector.memset(v_s[:].bitcast(I32), 0)

        offs_t = load_list(offs, "offs_t")
        nc.scalar.dma_start(tab_s[0:P:8, :].bitcast(I32), tab_scales[0].bitcast(I32))
        for q in range(4):
            nc.sync.dma_start(wb_s_raw[32 * q : 32 * q + 4, :].bitcast(I32), wb_scales[0, 4 * q : 4 * q + 4, :].bitcast(I32))
        wb_raw = keep.tile([P, 2 * H], U8, name="wb_raw", align_bytes=64)
        nc.sync.dma_start(wb_raw[:].bitcast(I32), wb_words[0].bitcast(I32))
        tab_w = keep.tile([P, T], I32, name="tab_w", align_bytes=64)
        nc.sync.dma_start(tab_w[:], tab_words[0].rearrange("p n i -> p (n i)").bitcast(I32))

        def load_wa(piece):
            raw = keep.tile([P, PACK, PIECE], F32, name="wa_raw", tag=f"stage{piece}")
            cols = slice(piece * PIECE, (piece + 1) * PIECE)
            nc.sync.dma_start(raw[:], wa[:, cols].rearrange("(p j) c -> p j c", j=PACK))
            return raw

        wa_raw = [load_wa(0), load_wa(1)]
        pos2_t = load_list(pos2, "pos2_t")
        pos1_t = load_list(pos1, "pos1_t")
        pos3_t = load_list(pos3, "pos3_t")
        thr_t = load_rows(thr, "thr_t")
        gt_t = load_rows(gt, "gt_t")
        gh_t = load_rows(gh, "gh_t")

        neg_bh = keep.tile([P, SLICES], F32, name="neg_bh")
        nc.scalar.activation(neg_bh[:], bh_t, ACT.Copy, scale=-1.0)

        wb_w = keep.tile([P, 2 * H], U8, name="wb_w", align_bytes=64)
        wb_s = keep.tile([P, H], U8, name="wb_s", align_bytes=64)
        nc.vector.tensor_copy(
            wb_w[:].bitcast(U16).rearrange("p (b t c i) -> p b c t i", b=BLOCKS, t=PACK, i=8),
            wb_raw[:].bitcast(U16).rearrange("p (b c i t) -> p b c t i", b=BLOCKS, t=PACK, i=8),
        )

        v_w = [keep.tile([P, BANK], U32, name=f"v_w{j}", align_bytes=64) for j in range(S // BANK)]
        nc.vector.tensor_copy(
            wb_s[:].rearrange("p (b t c i) -> p b c t i", b=BLOCKS, t=PACK, i=16),
            wb_s_raw[:].rearrange("p (b c i t) -> p b c t i", b=BLOCKS, t=PACK, i=16),
        )
        v_s_rows = keep.tile([P, S], U8, name="v_s_rows", align_bytes=64)
        nc.vector.tensor_copy(v_s_rows[:], tab_s[:].indirect(offs_t[:]))
        for q in range(4):
            nc.scalar.dma_start(v_s[32 * q : 32 * q + 4, :].bitcast(I32), v_s_rows[32 * q : 32 * q + 32 : 8, :].bitcast(I32))
        wy_s_raw = wb_s_raw
        for q in range(4):
            nc.gpsimd.dma_start(wy_s_raw[32 * q : 32 * q + 8, :].bitcast(I32), wy_scales[:, 4 * q : 4 * q + 4, :].bitcast(I32))
        cols_per_bank = BANK // LIST_ROWS
        for j in range(S // BANK):
            nc.vector.tensor_copy(
                v_w[j][:], tab_w[:].bitcast(U32).indirect(offs_t[:, j * cols_per_bank : (j + 1) * cols_per_bank])
            )

        wa_w = keep.tile([P, H], U32, name="wa_w", align_bytes=64)
        wa_s = keep.tile([P, H], U8, name="wa_s", align_bytes=64)
        wa_bf = [keep.tile([P, PACK, P, PACK], BF16, name="wa_bf", tag=f"wa_bf{b}", align_bytes=64) for b in range(BLOCKS)]

        def round_wa(piece, copy):
            b, half = divmod(piece, PASS // PIECE)
            qs = slice(half * PIECE // PACK, (half + 1) * PIECE // PACK)
            copy(
                wa_bf[b][:, :, qs, :].rearrange("p t q j -> p q t j"),
                wa_raw[piece][:].rearrange("p j (q t) -> p q t j", t=PACK),
            )

        def quantise_wa(b, t0, t1):
            cols = slice(b * PASS + t0 * P, b * PASS + t1 * P)
            nc.vector.quantize_mx(
                out=wa_w[:, cols].bitcast(E4M3X4), scales=wa_s[:, cols],
                in_=wa_bf[b][:, t0:t1].rearrange("p t q j -> p (t q j)"),
            )

        round_wa(0, nc.scalar.copy)
        round_wa(1, nc.vector.tensor_copy)
        quantise_wa(0, 0, 1)
        quantise_wa(0, 1, PACK)
        wy_s = keep.tile([P, H], U8, name="wy_s", tag="wa_bf0", align_bytes=64)
        nc.vector.tensor_copy(
            wy_s[:].rearrange("p (b t c i) -> p b c t i", b=BLOCKS, t=PACK, i=16),
            wy_s_raw[:].rearrange("p (b c i t) -> p b c t i", b=BLOCKS, t=PACK, i=16),
        )

        h = [keep.tile([P, S], F32, name=f"h{n}") for n in range(SLICES)]
        x_w1 = keep.tile([P, PAIRS], I32, name="x_w1", align_bytes=64)
        x_w = {1: x_w1[:]}
        x_s = [keep.tile([P, PAIRS], U8, name=f"x_s{b}", align_bytes=64) for b in range(BLOCKS)]
        whole = slice(0, PAIRS)
        parts = [slice(0, 256), slice(256, 384), slice(384, 512)]
        x_parts = [[whole], parts]
        x_pairs = {}
        x_il = {}
        for b in range(BLOCKS):
            for ms in x_parts[b]:
                width = ms.stop - ms.start
                x_pairs[(b, ms.start)] = keep.tile([P, 2, width, 2], BF16, name=f"x_pairs{b}_{ms.start}", align_bytes=64)
                x_il[(b, ms.start)] = keep.tile([P, width, PACK], BF16, name="x_il", tag=f"x_il{b}_{ms.start}", align_bytes=64)
        staged = {}
        picked = {}

        def products(n):
            cols = slice(n * P, (n + 1) * P)
            for j in range(S // BANK):
                js = slice(j * BANK, (j + 1) * BANK)
                hb_ps = psum.tile([P, BANK], F32, name="hb_ps", tag=f"hb{j}")
                nc.tensor.matmul_mx(
                    out=hb_ps[:], lhsT=wb_w[:, 2 * n * P : 2 * (n + 1) * P].bitcast(E2M1X4), lhsT_scale=wb_s[:, cols],
                    rhs=v_w[j][:].bitcast(E4M3X4), rhs_scale=v_s[:, js], start=True, stop=True,
                )
                lo_ps = psum.tile([P, BANK], F32, name="lo_ps", tag=f"lo{j}")
                nc.tensor.matmul_mx(
                    out=lo_ps[:], lhsT=wa_w[:, cols].bitcast(E4M3X4), lhsT_scale=wa_s[:, cols],
                    rhs=v_w[j][:].bitcast(E4M3X4), rhs_scale=v_s[:, js], start=True, stop=True,
                )
                if n == 0:
                    hb_sb = keep.tile([P, BANK], F32, name="hb_sb", tag=f"stage{2 + j}")
                else:
                    hb_sb = ring.tile([P, BANK], F32, name="hb_sb", tag=f"hb_sb{j}")
                nc.scalar.copy(hb_sb[:], hb_ps[:])
                staged[(n, j)] = (lo_ps, hb_sb)

        def join(n, j):
            lo, hb_sb = staged[(n, j)]
            dst = h[n][:, j * BANK : (j + 1) * BANK]
            nc.vector.scalar_tensor_tensor(dst, lo[:], thr_t[:, n : n + 1], hb_sb[:], ALU.max, ALU.subtract)

        def pair_tiles(n):
            if n == SLICES - 1:
                second = keep.tile([P, PAIRS], F32, name="second", tag="late_codes", align_bytes=64)
            else:
                second = ring.tile([P, PAIRS], F32, name="second", bufs=3)
            diff = ring.tile([P, PAIRS], F32, name="diff")
            if n >= SLICES - 2:
                bounded = keep.tile([P, PAIRS], F32, name="bounded", tag="late_page")
            else:
                bounded = ring.tile([P, PAIRS], F32, name="bounded")
            picked[n] = (second, diff, bounded)

        def list_cols(ms):
            return slice(ms.start // LIST_ROWS, ms.stop // LIST_ROWS)

        def pick_second(n, ms):
            nc.vector.tensor_copy(picked[n][0][:, ms], h[n][:].indirect(pos2_t[:, list_cols(ms)]))

        def pair(n, ms):
            b, t = divmod(n, PACK)
            second, diff, bounded = picked[n]
            if n >= FUSED_FROM:
                nc.vector.tensor_tensor(diff[:, ms], h[n][:].indirect(pos1_t[:, list_cols(ms)]), second[:, ms], ALU.subtract)
            else:
                first = ring.tile([P, PAIRS], F32, name="first", bufs=3)
                nc.vector.tensor_copy(first[:], h[n][:].indirect(pos1_t[:]))
                nc.gpsimd.tensor_tensor(diff[:], first[:], second[:], ALU.subtract)
            nc.scalar.activation(bounded[:, ms], diff[:, ms], ACT.Tanh)
            for part in x_parts[b]:
                if ms.start <= part.start < ms.stop:
                    nc.scalar.activation(
                        x_pairs[(b, part.start)][:, t // 2, :, t % 2], bounded[:, part], ACT.Copy, scale=gt_t[:, n : n + 1]
                    )

        def weave_x(b, ms, copy):
            copy(
                x_il[(b, ms.start)][:].bitcast(F32),
                x_pairs[(b, ms.start)][:].rearrange("p u m e -> p u (m e)").bitcast(F32).rearrange("p u m -> p m u"),
            )

        def quantise_x(b, ms):
            nc.vector.quantize_mx(
                out=x_w[b][:, ms].bitcast(E4M3X4), scales=x_s[b][:, ms],
                in_=x_il[(b, ms.start)][:].rearrange("p m t -> p (m t)"),
            )

        pages = {}

        def shift_h(n, js):
            if n == 5:
                pages[n] = keep.tile([P, PAIRS + S], F32, name="page", tag="late_page")
            if n not in pages:
                pages[n] = ring.tile([P, PAIRS + S], F32, name="page", bufs=5)
            dst = pages[n][:, PAIRS + js.start : PAIRS + js.stop]
            if n < SHIFTS_ON_GPSIMD:
                nc.gpsimd.tensor_scalar(
                    dst, h[n][:, js], gh_t[:, n : n + 1], neg_bh[:, n : n + 1], ALU.mult, ALU.add
                )
            else:
                nc.scalar.activation(
                    dst, h[n][:, js], ACT.Identity, bias=neg_bh[:, n : n + 1], scale=gh_t[:, n : n + 1]
                )

        row = slice(0, S)
        wy_w = {}

        def deal_wy(b):
            cols = slice(b * PASS, (b + 1) * PASS)
            for a in range(BLOCKS):
                nc.vector.tensor_copy(
                    wy_w[b][:, a, :].rearrange("p (t c i) -> p c t i", t=PACK, i=4),
                    wy_raw[a][:, cols].rearrange("p (c i t) -> p c t i", t=PACK, i=4),
                )

        wy_raw = []
        products(0)
        join(0, 0)
        join(0, 1)
        products(1)
        for a in range(BLOCKS):
            wa_raw.append(load_wa(2 + a))
            round_wa(2 + a, nc.scalar.copy)
            raw = keep.tile([P, H], I32, name="wy_raw", tag=f"stage{2 + a}")
            nc.sync.dma_start(raw[:], wy_words[a].rearrange("p c i -> p (c i)").bitcast(I32))
            wy_raw.append(raw)
        for n in range(SLICES):
            pair_tiles(n)
            if n + 2 < SLICES:
                products(n + 2)
            if n + 1 < SLICES:
                join(n + 1, 0)
                pick_second(n, whole)
                join(n + 1, 1)
                pair(n, whole)
            else:
                pick_second(n, parts[0])
                pick_second(n, parts[1])
                pair(n, parts[0])
                pair(n, parts[1])
                pick_second(n, parts[2])
                pair(n, parts[2])
            if n == 0:
                quantise_wa(1, 0, PACK)
            if n == WEAVE_AT:
                weave_x(0, whole, nc.scalar.copy)
            if n < 5:
                shift_h(n, row)

        shift_h(5, row)
        late = keep.tile([P, 1 + BLOCKS, PASS], I32, name="late", tag="late_codes", align_bytes=64)
        x_w[0] = late[:, 0, :]
        wy_w[0] = late[:, 1:, :]
        quantise_x(0, whole)
        deal_wy(0)
        weave_x(1, parts[0], nc.vector.tensor_copy)
        weave_x(1, parts[1], nc.vector.tensor_copy)
        quantise_x(1, parts[0])
        weave_x(1, parts[2], nc.vector.tensor_copy)
        quantise_x(1, parts[1])
        quantise_x(1, parts[2])
        wy_w1 = keep.tile([P, BLOCKS, PASS], I32, name="wy_w1", tag=f"x_il1_{parts[2].start}", align_bytes=64)
        wy_w[1] = wy_w1[:]
        deal_wy(1)

        out_rows = out.rearrange("(b p t) j -> b t p j", b=BLOCKS, t=PACK)
        lifted = {}

        def second_stage(n):
            cols = slice(n * P, (n + 1) * P)
            page = pages[n]
            b, t = divmod(n, PACK)
            if n == 0:
                pieces = list(zip(parts, ("hb0", "lo0", "lo0"), [(0, 1)] * 3))
            else:
                pieces = [(whole, "lo0", (1, 0))]
            for ms, bank, passes in pieces:
                y_ps = psum.tile([P, BANK], F32, name="y_ps", tag=bank)
                width = ms.stop - ms.start
                for a in passes:
                    nc.tensor.matmul_mx(
                        out=y_ps[:, :width], lhsT=wy_w[b][:, a, t * P : (t + 1) * P].bitcast(E4M3X4),
                        lhsT_scale=wy_s[4 * a : P, cols],
                        rhs=x_w[a][:, ms].bitcast(E4M3X4), rhs_scale=x_s[a][:, ms],
                        start=(a == passes[0]), stop=(a == passes[-1]),
                    )
                copy = nc.vector.tensor_copy if n == 0 and ms != parts[0] else nc.scalar.copy
                copy(page[:, ms], y_ps[:, :width])

        def lift(n, js):
            up = lifted[n]
            nc.vector.tensor_copy(up[:, js], pages[n][:].indirect(pos3_t[:, list_cols(js)]))
            nc.scalar.activation(up[:, js], up[:, js], ACT.Sigmoid)

        def finish(n, js, engine):
            b, t = divmod(n, PACK)
            up = lifted[n]
            engine.tensor_tensor(up[:, js], up[:, js], pages[n][:, PAIRS + js.start : PAIRS + js.stop], ALU.mult)
            nc.sync.dma_start(out_rows[b, t, :, js], up[:, js])

        last_parts = [slice(0, 512), slice(512, 768), slice(768, 1024)]
        first_parts = [slice(0, 256), slice(256, S)]
        second_stage(0)
        for n in range(SLICES):
            lifted[n] = ring.tile([P, S], F32, name="up", bufs=4)
            if n + 1 < SLICES:
                second_stage(n + 1)
                if 2 <= n < 6:
                    late, half = divmod(n - 2, 2)
                    shift_h(6 + late, slice(half * BANK, (half + 1) * BANK))
                for js in (first_parts if n == 0 else (slice(0, BANK), slice(BANK, S))):
                    lift(n, js)
                if n + 2 < SLICES:
                    finish(n, row, nc.gpsimd)

                else:
                    finish(n, slice(0, BANK), nc.gpsimd)
            else:
                for js in last_parts:
                    lift(n, js)
                finish(n - 1, slice(BANK, S), nc.vector)
                for js in last_parts:
                    finish(n, js, nc.vector)
